import numpy as np
import ml_dtypes


def mxq(x, axis, fmt="e4m3"):
    dtype, down = {"e4m3": (ml_dtypes.float8_e4m3fn, 7), "e5m2": (ml_dtypes.float8_e5m2, 14)}[fmt]
    v = np.moveaxis(np.asarray(x, np.float32).astype(ml_dtypes.bfloat16).astype(np.float64), axis, -1)
    blocks = v.reshape(v.shape[:-1] + (-1, 32))
    amax = np.abs(blocks).max(-1, keepdims=True)
    byte = np.maximum(np.where(amax > 0, np.frexp(amax)[1] - 1 + 127, 0) - down, 1)
    scale = np.exp2(byte - 127.0)
    codes = (blocks / scale).astype(np.float32).astype(dtype).astype(np.float64)
    return np.moveaxis((codes * scale).reshape(v.shape), -1, axis)


WIDE = False


def mx_kscale(k):
    if not WIDE:
        return np.ones(k)
    levels = np.array([10, -10, 5, -5, 0])
    if k % 512:
        return np.exp2(np.random.permutation(np.resize(levels, k // 32))).repeat(32)
    a = np.empty((k // 512, 16))
    for p in range(k // 512):
        a[p, :8] = np.random.permutation(np.resize(levels, 8))
        for g in range(8):
            far = levels[np.abs(levels - a[p, g]) >= 10]
            a[p, g + 8] = far[np.random.randint(len(far))]
    return np.exp2(a.ravel()).repeat(32)


def f64(x):
    return np.asarray(x).astype(np.float64)


def striped(idx):
    return np.tile(np.asarray(idx).reshape(-1, 16).T, (8, 1)).astype(np.uint16)


def unstriped(offs):
    return offs[:16].T.reshape(-1).astype(np.int64)


E2M1 = np.array([0.0, 0.5, 1.0, 1.5, 2.0, 3.0, 4.0, 6.0, -0.0, -0.5, -1.0, -1.5, -2.0, -3.0, -4.0, -6.0])


def pack_weight(w, fmt):
    k, n = w.shape
    w = f64(np.asarray(w, np.float32).astype(ml_dtypes.bfloat16)).reshape(k // 32, 32, n)
    amax = np.abs(w).max(1)
    if fmt == "e4m3":
        byte = np.frexp(amax)[1] - 1 + 127 - 7
    else:
        mant, ex = np.frexp(amax / 6.0)
        byte = np.where(mant > 0.5, ex, ex - 1) + 127
    byte = np.clip(np.where(amax > 0, byte, 1), 1, 254)
    scaled = (w * np.exp2(127.0 - byte)[:, None, :]).reshape(k, n).astype(np.float32)
    by_word = np.ascontiguousarray(scaled.reshape(k // 512, 128, 4, n).transpose(0, 1, 3, 2))
    if fmt == "e4m3":
        words = by_word.astype(ml_dtypes.float8_e4m3fn).view(np.uint8)
    else:
        c = by_word.astype(ml_dtypes.float4_e2m1fn).view(np.uint8) & 0xF
        words = (c[..., 0::2] | (c[..., 1::2] << 4)).reshape(k // 512, 128, 2 * n)
    return np.ascontiguousarray(words), np.ascontiguousarray(byte.astype(np.uint8).reshape(k // 512, 16, n))


def unpack_weight(words, scales, fmt):
    g, _, n = scales.shape
    words = np.ascontiguousarray(words).reshape(g, 128, n, -1)
    if fmt == "e4m3":
        vals = words.view(ml_dtypes.float8_e4m3fn).astype(np.float64)
    else:
        nib = np.empty((g, 128, n, 4), np.uint8)
        nib[..., 0::2] = words & 0xF
        nib[..., 1::2] = words >> 4
        vals = E2M1[nib]
    vals = vals * np.repeat(np.exp2(scales.astype(np.float64) - 127.0), 8, axis=1)[..., None]
    return vals.transpose(0, 1, 3, 2).reshape(g * 512, n)


def sigmoid(v):
    return 1.0 / (1.0 + np.exp(-v))


D, T, I, Q, E, U, M = 512, 2048, 512, 256, 512, 1024, 1024


def setup_inputs():
    n = np.random.standard_normal
    idx = np.random.permutation(T)[:I]
    idx2 = np.random.permutation(U)[:I]
    idx3 = np.random.permutation(M)[:Q]
    fd = mx_kscale(D)
    fi = mx_kscale(I)
    ti = np.ones(T)
    ti[idx] = fi
    keysp = pack_weight(n((D, T)) / fd[:, None], "e2m1")
    return {
        "query": (n((D, Q)) * 0.7 / np.sqrt(D) * fd[:, None]).astype(np.float32),
        "query2": (n((D, Q)) * 0.7 / np.sqrt(D) * fd[:, None]).astype(np.float32),
        "keys_words": keysp[0],
        "keys_scales": keysp[1],
        "notes": (n((D, U)) / fd[:, None]).astype(np.float32),
        "os": (np.random.uniform(0.02, 0.08, (1, I)) * fi).astype(np.float32),
        "vals": (n((E, T)) / ti).astype(np.float32),
        "old": (n((E, M)) * 0.7).astype(np.float32),
        "offs": striped(idx),
        "offs2": striped(idx2),
        "offs3": striped(idx3),
    }


def reference(query, query2, keys_words, keys_scales, notes, os, vals, old, offs, offs2, offs3):
    idx = unstriped(offs)
    idx2 = unstriped(offs2)
    idx3 = unstriped(offs3)
    keysu = unpack_weight(keys_words, keys_scales, "e2m1")
    queryq = mxq(f64(query), 0, "e4m3")
    keysidxg = keysu[:, idx]
    query2q = mxq(f64(query2), 0, "e4m3")
    notesidx2q = mxq(f64(notes)[:, idx2], 0, "e4m3")
    s = queryq.T @ keysidxg + query2q.T @ notesidx2q
    w = sigmoid(s)
    wo1 = w * f64(os)
    wt1 = wo1.T
    vt1 = f64(vals)[:, idx].T
    vt1q = mxq(vt1, 0, "e4m3")
    wt1q = mxq(wt1, 0, "e4m3")
    o = vt1q.T @ wt1q
    of = np.zeros((E, M))
    of[:, idx3] = o
    y = np.maximum(of, f64(old)) + f64(old) * 0.25
    return y

@@ -1,0 +1,262 @@
+from contextlib import ExitStack
+
+import concourse.mybir as mybir
+from concourse.masks import make_identity
+
+D, T, I, Q, E, U, M = 512, 2048, 512, 256, 512, 1024, 1024
+FLOPS = 2 * (2 * D * Q * I) + 2 * I * E * Q
+
+F32 = mybir.dt.float32
+BF16 = mybir.dt.bfloat16
+I32 = mybir.dt.int32
+U32 = mybir.dt.uint32
+U16 = mybir.dt.uint16
+U8 = mybir.dt.uint8
+FP8X4 = mybir.dt.float8_e4m3fn_x4
+FP4X4 = mybir.dt.float4_e2m1fn_x4
+ALU = mybir.AluOpType
+ACT = mybir.ActivationFunctionType
+
+P = 128
+PACK = 4
+BLOCKS = E // P
+HALVES = Q // P
+
+
+def tile_attend_twosources_keptlarger_lean_kernel(
+    tc, query, query2, keys_words, keys_scales, notes, slot_os, vals, old, offs, offs2, offs3, out
+):
+    nc = tc.nc
+    with ExitStack() as ctx:
+        keep = ctx.enter_context(tc.tile_pool(name="keep", bufs=1))
+        psum = ctx.enter_context(tc.psum_pool(name="psum", bufs=1))
+
+        def sb(name, shape, dtype, tag=None):
+            return keep.tile(shape, dtype, name=name, tag=tag or name, align_bytes=64)
+
+        token_list = sb("token_list", [P, I // 16], U16)
+        note_list = sb("note_list", [P, I // 16], U16)
+        column_list = sb("column_list", [P, Q // 16], U16)
+        key_words = sb("key_words", [P, T], U16)
+        key_bytes = sb("key_bytes", [P, T], U8)
+        note_pool = [sb(f"note_pool{t}", [P, U], F32) for t in range(PACK)]
+        q_raw = [sb(f"q_raw{n}", [P, PACK, Q], F32) for n in range(2)]
+        slot_factor = sb("slot_factor", [P, PACK], F32)
+        val_pool = [sb(f"val_pool{b}", [P, T], F32) for b in range(BLOCKS)]
+        old_rows = [sb(f"old_rows{b}", [P, M], F32) for b in range(BLOCKS)]
+        placed = [sb(f"placed{n}", [P, M], F32) for n in range(2)]
+        identity = sb("identity", [P, P], F32)
+
+        nc.gpsimd.memset(key_bytes[:].bitcast(I32), 0)
+        make_identity(nc, identity[:])
+
+        notes_by_place = notes.rearrange("(p t) u -> t p u", t=PACK)
+        nc.sync.dma_start(key_words[:].bitcast(I32), keys_words[0].bitcast(I32))
+        nc.sync.dma_start(token_list[:], offs)
+        nc.sync.dma_start(note_pool[0][:], notes_by_place[0])
+        for quad in range(4):
+            nc.sync.dma_start(
+                key_bytes[32 * quad : 32 * quad + 4, :].bitcast(I32),
+                keys_scales[0, 4 * quad : 4 * quad + 4, :].bitcast(I32),
+            )
+        nc.sync.dma_start(note_pool[1][:], notes_by_place[1])
+        nc.sync.dma_start(note_list[:], offs2)
+        nc.sync.dma_start(note_pool[2][:], notes_by_place[2])
+        nc.sync.dma_start(note_pool[3][:], notes_by_place[3])
+        for n, source in enumerate((query, query2)):
+            nc.sync.dma_start(q_raw[n][:], source.rearrange("(p t) q -> p t q", t=PACK))
+        nc.sync.dma_start(slot_factor[:], slot_os.rearrange("o (p r) -> (o p) r", r=PACK))
+        nc.sync.dma_start(column_list[:], offs3)
+
+        def load_vals(b):
+            nc.sync.dma_start(val_pool[b][:], vals[b * P : (b + 1) * P, :])
+
+        def load_old(b):
+            nc.sync.dma_start(old_rows[b][:], old[b * P : (b + 1) * P, :])
+
+        load_vals(0)
+        load_vals(1)
+        load_vals(2)
+        load_vals(3)
+        load_old(0)
+        load_old(1)
+        load_old(2)
+        load_old(3)
+
+        for window in placed:
+            nc.vector.memset(window[:], 0.0)
+
+        got_words = sb("got_words", [P, I], U16)
+        key_codes = sb("key_codes", [P, I], U16)
+        key_scale = sb("key_scale", [P, I], U8)
+        nc.vector.tensor_copy(got_words[:], key_words[:].indirect(token_list[:]))
+        nc.vector.tensor_copy(
+            key_codes[:].rearrange("p (r s) -> p r s", r=PACK), got_words[:].rearrange("p (s r) -> p r s", r=PACK)
+        )
+        nc.vector.tensor_copy(
+            key_scale[:].rearrange("p (r s) -> p s r", r=PACK), key_bytes[:].indirect(token_list[:])
+        )
+
+        got_notes = sb("got_notes", [P, PACK, I], BF16)
+        for t in range(PACK):
+            listed = note_pool[t][:].indirect(note_list[:])
+            if t >= 2:
+                nc.vector.tensor_copy(got_notes[:, t, :], listed)
+            else:
+                nc.scalar.activation(got_notes[:, t, :], listed, ACT.Copy)
+        note_bf = sb("note_bf", [P, I * PACK], BF16)
+        note_codes = sb("note_codes", [P, I], U32)
+        note_scale = sb("note_scale", [P, I], U8)
+
+        q_bf = [sb(f"q_bf{n}", [P, Q * PACK], BF16) for n in range(2)]
+        q_codes = [sb(f"q_codes{n}", [P, Q], U32) for n in range(2)]
+        q_scale = [sb(f"q_scale{n}", [P, Q], U8) for n in range(2)]
+        nc.scalar.copy(
+            q_bf[0][:].rearrange("p (c i t) -> p c t i", i=4, t=PACK),
+            q_raw[0][:].rearrange("p t (c i) -> p c t i", i=4),
+        )
+        nc.vector.tensor_copy(
+            note_bf[:].rearrange("p (r s t) -> p r s t", r=PACK, t=PACK),
+            got_notes[:].rearrange("p t (s r) -> p r s t", r=PACK),
+        )
+        nc.vector.quantize_mx(q_codes[0][:].bitcast(FP8X4), q_scale[0][:], q_bf[0][:])
+        nc.scalar.copy(
+            q_bf[1][:].rearrange("p (c i t) -> p c t i", i=4, t=PACK),
+            q_raw[1][:].rearrange("p t (c i) -> p c t i", i=4),
+        )
+        nc.vector.quantize_mx(note_codes[:].bitcast(FP8X4), note_scale[:], note_bf[:])
+        nc.vector.quantize_mx(q_codes[1][:].bitcast(FP8X4), q_scale[1][:], q_bf[1][:])
+
+        val_bf = [sb(f"val_bf{b}", [P, P * PACK], BF16) for b in range(BLOCKS)]
+        val_scale = [sb(f"val_scale{b}", [P, P], U8) for b in range(BLOCKS)]
+        val_codes = {}
+        turned = {}
+        turn_banks = ("scores0", "scores1", "turned2", "turned3")
+
+        def gather_values(b, on_scalar, reuse):
+            got_vals = sb(f"got_vals{b}", [P, I], BF16, tag=reuse)
+            listed = val_pool[b][:].indirect(token_list[:])
+            if on_scalar:
+                nc.scalar.activation(got_vals[:], listed, ACT.Copy)
+            else:
+                nc.vector.tensor_copy(got_vals[:], listed)
+            return got_vals
+
+        def turn_values(b, got_vals):
+            pairs = got_vals[:].bitcast(F32)
+            turned[b] = psum.tile([P, 2, P], F32, name=f"turned{b}", tag=turn_banks[b])
+            for u in range(2):
+                nc.tensor.transpose(turned[b][:, u, :], pairs[:, u : I // 2 : 2], identity[:])
+
+        def weave_values(b, on_scalar):
+            woven = val_bf[b][:].bitcast(F32).rearrange("p (e u) -> p e u", u=2)
+            if on_scalar:
+                nc.scalar.copy(woven, turned[b][:].rearrange("p u e -> p e u"))
+            else:
+                nc.vector.tensor_copy(woven, turned[b][:].rearrange("p u e -> p e u"))
+
+        def quantise_values(b, reuse=None):
+            val_codes[b] = sb(f"val_codes{b}", [P, P], U32, tag=reuse)
+            nc.vector.quantize_mx(val_codes[b][:].bitcast(FP8X4), val_scale[b][:], val_bf[b][:])
+
+        weight = sb("weight", [P, Q, PACK], F32)
+        weight_codes = sb("weight_codes", [P, Q], U32)
+        weight_scale = sb("weight_scale", [P, Q], U8)
+        scores = [psum.tile([P, PACK, P], F32, name=f"scores{h}", tag=f"scores{h}") for h in range(HALVES)]
+        for h in range(HALVES):
+            rows = slice(h * P, (h + 1) * P)
+            for r in range(PACK):
+                slots = slice(r * P, (r + 1) * P)
+                nc.tensor.matmul_mx(
+                    scores[h][:, r, :],
+                    lhsT=key_codes[:, slots].bitcast(FP4X4),
+                    lhsT_scale=key_scale[:, slots],
+                    rhs=q_codes[0][:, rows].bitcast(FP8X4),
+                    rhs_scale=q_scale[0][:, rows],
+                    start=(r == 0),
+                    stop=False,
+                )
+        got0 = gather_values(0, False, "q_bf1")
+        weight_bf = sb("weight_bf", [P, Q, PACK], BF16, tag="val_pool0")
+        for h in range(HALVES):
+            rows = slice(h * P, (h + 1) * P)
+            for r in range(PACK):
+                slots = slice(r * P, (r + 1) * P)
+                nc.tensor.matmul_mx(
+                    scores[h][:, r, :],
+                    lhsT=note_codes[:, slots].bitcast(FP8X4),
+                    lhsT_scale=note_scale[:, slots],
+                    rhs=q_codes[1][:, rows].bitcast(FP8X4),
+                    rhs_scale=q_scale[1][:, rows],
+                    start=False,
+                    stop=(r == PACK - 1),
+                )
+            nc.scalar.activation(weight[:, rows, :], scores[h][:].rearrange("p r q -> p q r"), ACT.Sigmoid)
+            nc.vector.tensor_tensor(
+                weight_bf[:, rows, :],
+                weight[:, rows, :],
+                slot_factor[:].unsqueeze(1).to_broadcast([P, P, PACK]),
+                ALU.mult,
+            )
+        turn_values(0, got0)
+        weave_values(0, True)
+        quantise_values(0)
+        nc.vector.quantize_mx(
+            weight_codes[:].bitcast(FP8X4), weight_scale[:], weight_bf[:].rearrange("p q r -> p (q r)")
+        )
+
+        result = [sb(f"result{b}", [P, M], F32) for b in range(BLOCKS)]
+        read = {}
+
+        def read_values(b, reuse=None):
+            sums = psum.tile([P, Q], F32, name=f"sums{b}", tag=f"sums{b % 2}")
+            nc.tensor.matmul_mx(
+                sums[:],
+                lhsT=val_codes[b][:].bitcast(FP8X4),
+                lhsT_scale=val_scale[b][:],
+                rhs=weight_codes[:].bitcast(FP8X4),
+                rhs_scale=weight_scale[:],
+                start=True,
+                stop=True,
+            )
+            read[b] = sb(f"read{b}", [P, Q], F32, tag=reuse)
+            nc.scalar.copy(read[b][:], sums[:])
+
+        def place(b):
+            nc.scalar.activation(placed[b % 2][:].indirect(column_list[:]), read[b][:], ACT.Copy)
+
+        def update(b, store_parts):
+            parts = [slice(0, M // 2), slice(M // 2, M)]
+            larger = [sb(f"larger{b}_{n}", [P, M // 2], F32) for n in range(2)]
+            for n, cols in enumerate(parts):
+                nc.vector.tensor_tensor(larger[n][:], placed[b % 2][:, cols], old_rows[b][:, cols], ALU.max)
+            for n, cols in enumerate(parts):
+                nc.vector.scalar_tensor_tensor(
+                    result[b][:, cols], old_rows[b][:, cols], 0.25, larger[n][:], ALU.mult, ALU.add
+                )
+                if store_parts:
+                    nc.sync.dma_start(out[b * P : (b + 1) * P, cols], result[b][:, cols])
+            if not store_parts:
+                nc.sync.dma_start(out[b * P : (b + 1) * P, :], result[b][:])
+
+        turn_values(1, gather_values(1, True, "note_codes"))
+        read_values(0, "val_pool1")
+        place(0)
+        weave_values(1, False)
+        quantise_values(1)
+        turn_values(2, gather_values(2, False, "val_pool0"))
+        read_values(1)
+        place(1)
+        weave_values(2, True)
+        turn_values(3, gather_values(3, False, None))
+        update(0, False)
+        quantise_values(2, "larger0_0")
+        read_values(2)
+        weave_values(3, True)
+        place(2)
+        update(1, False)
+        quantise_values(3, "larger1_0")
+        read_values(3)
+        place(3)
+        update(2, False)
+        update(3, True)

@@ -100,12 +100,11 @@ def tile_attend_twosources_keptlarger_lean_kernel(
         got_notes = sb("got_notes", [P, PACK, I], BF16)
         for t in range(PACK):
             listed = note_pool[t][:].indirect(note_list[:])
-            if t >= 2:
+            if t % 2 == 1:
                 nc.vector.tensor_copy(got_notes[:, t, :], listed)
             else:
                 nc.scalar.activation(got_notes[:, t, :], listed, ACT.Copy)
         note_bf = sb("note_bf", [P, I * PACK], BF16)
-        note_codes = sb("note_codes", [P, I], U32)
         note_scale = sb("note_scale", [P, I], U8)
 
         q_bf = [sb(f"q_bf{n}", [P, Q * PACK], BF16) for n in range(2)]
@@ -120,10 +119,11 @@ def tile_attend_twosources_keptlarger_lean_kernel(
             got_notes[:].rearrange("p t (s r) -> p r s t", r=PACK),
         )
         nc.vector.quantize_mx(q_codes[0][:].bitcast(FP8X4), q_scale[0][:], q_bf[0][:])
-        nc.scalar.copy(
+        nc.vector.tensor_copy(
             q_bf[1][:].rearrange("p (c i t) -> p c t i", i=4, t=PACK),
             q_raw[1][:].rearrange("p t (c i) -> p c t i", i=4),
         )
+        note_codes = sb("note_codes", [P, I], U32, tag="q_raw1")
         nc.vector.quantize_mx(note_codes[:].bitcast(FP8X4), note_scale[:], note_bf[:])
         nc.vector.quantize_mx(q_codes[1][:].bitcast(FP8X4), q_scale[1][:], q_bf[1][:])
 
@@ -230,16 +230,20 @@ def tile_attend_twosources_keptlarger_lean_kernel(
             larger = [sb(f"larger{b}_{n}", [P, M // 2], F32) for n in range(2)]
             for n, cols in enumerate(parts):
                 nc.vector.tensor_tensor(larger[n][:], placed[b % 2][:, cols], old_rows[b][:, cols], ALU.max)
-            for n, cols in enumerate(parts):
+            ends = (M // 2, 3 * M // 4, M) if store_parts else (M // 2, M)
+            for first, end in zip((0,) + ends, ends):
+                cols = slice(first, end)
+                n = first // (M // 2)
+                within = slice(first - n * (M // 2), end - n * (M // 2))
                 nc.vector.scalar_tensor_tensor(
-                    result[b][:, cols], old_rows[b][:, cols], 0.25, larger[n][:], ALU.mult, ALU.add
+                    result[b][:, cols], old_rows[b][:, cols], 0.25, larger[n][:, within], ALU.mult, ALU.add
                 )
                 if store_parts:
                     nc.sync.dma_start(out[b * P : (b + 1) * P, cols], result[b][:, cols])
             if not store_parts:
                 nc.sync.dma_start(out[b * P : (b + 1) * P, :], result[b][:])
 
-        turn_values(1, gather_values(1, True, "note_codes"))
+        turn_values(1, gather_values(1, True, "q_raw1"))
         read_values(0, "val_pool1")
         place(0)
         weave_values(1, False)

@@ -65,8 +65,6 @@ def tile_attend_twosources_keptlarger_lean_kernel(
         nc.sync.dma_start(note_pool[3][:], notes_by_place[3])
         for n, source in enumerate((query, query2)):
             nc.sync.dma_start(q_raw[n][:], source.rearrange("(p t) q -> p t q", t=PACK))
-        nc.sync.dma_start(slot_factor[:], slot_os.rearrange("o (p r) -> (o p) r", r=PACK))
-        nc.sync.dma_start(column_list[:], offs3)
 
         def load_vals(b):
             nc.sync.dma_start(val_pool[b][:], vals[b * P : (b + 1) * P, :])
@@ -75,6 +73,8 @@ def tile_attend_twosources_keptlarger_lean_kernel(
             nc.sync.dma_start(old_rows[b][:], old[b * P : (b + 1) * P, :])
 
         load_vals(0)
+        nc.sync.dma_start(slot_factor[:], slot_os.rearrange("o (p r) -> (o p) r", r=PACK))
+        nc.sync.dma_start(column_list[:], offs3)
         load_vals(1)
         load_vals(2)
         load_vals(3)
@@ -91,7 +91,8 @@ def tile_attend_twosources_keptlarger_lean_kernel(
         key_scale = sb("key_scale", [P, I], U8)
         nc.vector.tensor_copy(got_words[:], key_words[:].indirect(token_list[:]))
         nc.vector.tensor_copy(
-            key_codes[:].rearrange("p (r s) -> p r s", r=PACK), got_words[:].rearrange("p (s r) -> p r s", r=PACK)
+            key_codes[:].rearrange("p (r g s) -> p g r s", r=PACK, s=8),
+            got_words[:].rearrange("p (g s r) -> p g r s", s=8, r=PACK),
         )
         nc.vector.tensor_copy(
             key_scale[:].rearrange("p (r s) -> p s r", r=PACK), key_bytes[:].indirect(token_list[:])
@@ -115,19 +116,20 @@ def tile_attend_twosources_keptlarger_lean_kernel(
             q_raw[0][:].rearrange("p t (c i) -> p c t i", i=4),
         )
         nc.vector.tensor_copy(
-            note_bf[:].rearrange("p (r s t) -> p r s t", r=PACK, t=PACK),
-            got_notes[:].rearrange("p t (s r) -> p r s t", r=PACK),
+            note_bf[:].rearrange("p (r g s t) -> p g r s t", r=PACK, s=2, t=PACK),
+            got_notes[:].rearrange("p t (g s r) -> p g r s t", s=2, r=PACK),
         )
+        for copy, first in ((nc.vector.tensor_copy, 0), (nc.scalar.copy, P)):
+            copy(
+                q_bf[1][:, first * PACK : (first + P) * PACK].rearrange("p (c i t) -> p c t i", i=4, t=PACK),
+                q_raw[1][:, :, first : first + P].rearrange("p t (c i) -> p c t i", i=4),
+            )
         nc.vector.quantize_mx(q_codes[0][:].bitcast(FP8X4), q_scale[0][:], q_bf[0][:])
-        nc.vector.tensor_copy(
-            q_bf[1][:].rearrange("p (c i t) -> p c t i", i=4, t=PACK),
-            q_raw[1][:].rearrange("p t (c i) -> p c t i", i=4),
-        )
-        note_codes = sb("note_codes", [P, I], U32, tag="q_raw1")
+        note_codes = sb("note_codes", [P, I], U32, tag="q_bf0")
         nc.vector.quantize_mx(note_codes[:].bitcast(FP8X4), note_scale[:], note_bf[:])
         nc.vector.quantize_mx(q_codes[1][:].bitcast(FP8X4), q_scale[1][:], q_bf[1][:])
 
-        val_bf = [sb(f"val_bf{b}", [P, P * PACK], BF16) for b in range(BLOCKS)]
+        val_bf = {}
         val_scale = [sb(f"val_scale{b}", [P, P], U8) for b in range(BLOCKS)]
         val_codes = {}
         turned = {}
@@ -148,7 +150,8 @@ def tile_attend_twosources_keptlarger_lean_kernel(
             for u in range(2):
                 nc.tensor.transpose(turned[b][:, u, :], pairs[:, u : I // 2 : 2], identity[:])
 
-        def weave_values(b, on_scalar):
+        def weave_values(b, on_scalar, reuse=None):
+            val_bf[b] = sb(f"val_bf{b}", [P, P * PACK], BF16, tag=reuse)
             woven = val_bf[b][:].bitcast(F32).rearrange("p (e u) -> p e u", u=2)
             if on_scalar:
                 nc.scalar.copy(woven, turned[b][:].rearrange("p u e -> p e u"))
@@ -243,23 +246,23 @@ def tile_attend_twosources_keptlarger_lean_kernel(
             if not store_parts:
                 nc.sync.dma_start(out[b * P : (b + 1) * P, :], result[b][:])
 
-        turn_values(1, gather_values(1, True, "q_raw1"))
+        turn_values(1, gather_values(1, True, "q_bf0"))
         read_values(0, "val_pool1")
         place(0)
-        weave_values(1, False)
-        quantise_values(1)
         turn_values(2, gather_values(2, False, "val_pool0"))
-        read_values(1)
-        place(1)
+        weave_values(1, False, "val_pool2")
+        quantise_values(1)
         weave_values(2, True)
+        read_values(1, "val_pool0")
+        place(1)
         turn_values(3, gather_values(3, False, None))
-        update(0, False)
-        quantise_values(2, "larger0_0")
-        read_values(2)
+        quantise_values(2, "val_pool3")
         weave_values(3, True)
+        read_values(2, "got_vals3")
+        update(0, False)
         place(2)
+        quantise_values(3, "larger0_1")
         update(1, False)
-        quantise_values(3, "larger1_0")
         read_values(3)
         place(3)
         update(2, False)

from contextlib import ExitStack

import concourse.mybir as mybir
from concourse.masks import make_identity

D, T, I, Q, E, U, M = 512, 2048, 512, 256, 512, 1024, 1024
FLOPS = 2 * (2 * D * Q * I) + 2 * I * E * Q

F32 = mybir.dt.float32
BF16 = mybir.dt.bfloat16
I32 = mybir.dt.int32
U32 = mybir.dt.uint32
U16 = mybir.dt.uint16
U8 = mybir.dt.uint8
FP8X4 = mybir.dt.float8_e4m3fn_x4
FP4X4 = mybir.dt.float4_e2m1fn_x4
ALU = mybir.AluOpType
ACT = mybir.ActivationFunctionType

P = 128
PACK = 4
BLOCKS = E // P
HALVES = Q // P


def tile_attend_twosources_keptlarger_lean_kernel(
    tc, query, query2, keys_words, keys_scales, notes, slot_os, vals, old, offs, offs2, offs3, out
):
    nc = tc.nc
    with ExitStack() as ctx:
        keep = ctx.enter_context(tc.tile_pool(name="keep", bufs=1))
        psum = ctx.enter_context(tc.psum_pool(name="psum", bufs=1))

        def sb(name, shape, dtype, tag=None):
            return keep.tile(shape, dtype, name=name, tag=tag or name, align_bytes=64)

        token_list = sb("token_list", [P, I // 16], U16)
        note_list = sb("note_list", [P, I // 16], U16)
        column_list = sb("column_list", [P, Q // 16], U16)
        key_words = sb("key_words", [P, T], U16)
        key_bytes = sb("key_bytes", [P, T], U8)
        note_pool = [sb(f"note_pool{t}", [P, U], F32) for t in range(PACK)]
        q_raw = [sb(f"q_raw{n}", [P, PACK, Q], F32) for n in range(2)]
        slot_factor = sb("slot_factor", [P, PACK], F32)
        val_pool = [sb(f"val_pool{b}", [P, T], F32) for b in range(BLOCKS)]
        old_rows = [sb(f"old_rows{b}", [P, M], F32) for b in range(BLOCKS)]
        placed = [sb(f"placed{n}", [P, M], F32) for n in range(2)]
        identity = sb("identity", [P, P], F32)

        nc.gpsimd.memset(key_bytes[:].bitcast(I32), 0)
        make_identity(nc, identity[:])

        notes_by_place = notes.rearrange("(p t) u -> t p u", t=PACK)
        nc.sync.dma_start(key_words[:].bitcast(I32), keys_words[0].bitcast(I32))
        nc.sync.dma_start(token_list[:], offs)
        nc.sync.dma_start(note_pool[0][:], notes_by_place[0])
        for quad in range(4):
            nc.sync.dma_start(
                key_bytes[32 * quad : 32 * quad + 4, :].bitcast(I32),
                keys_scales[0, 4 * quad : 4 * quad + 4, :].bitcast(I32),
            )
        nc.sync.dma_start(note_pool[1][:], notes_by_place[1])
        nc.sync.dma_start(note_list[:], offs2)
        nc.sync.dma_start(note_pool[2][:], notes_by_place[2])
        nc.sync.dma_start(note_pool[3][:], notes_by_place[3])
        for n, source in enumerate((query, query2)):
            nc.sync.dma_start(q_raw[n][:], source.rearrange("(p t) q -> p t q", t=PACK))

        def load_vals(b):
            nc.sync.dma_start(val_pool[b][:], vals[b * P : (b + 1) * P, :])

        def load_old(b):
            nc.sync.dma_start(old_rows[b][:], old[b * P : (b + 1) * P, :])

        load_vals(0)
        nc.sync.dma_start(slot_factor[:], slot_os.rearrange("o (p r) -> (o p) r", r=PACK))
        nc.sync.dma_start(column_list[:], offs3)
        load_vals(1)
        load_vals(2)
        load_vals(3)
        load_old(0)
        load_old(1)
        load_old(2)
        load_old(3)

        for window in placed:
            nc.vector.memset(window[:], 0.0)

        got_words = sb("got_words", [P, I], U16)
        key_codes = sb("key_codes", [P, I], U16)
        key_scale = sb("key_scale", [P, I], U8)
        nc.vector.tensor_copy(got_words[:], key_words[:].indirect(token_list[:]))
        nc.vector.tensor_copy(
            key_codes[:].rearrange("p (r g s) -> p g r s", r=PACK, s=8),
            got_words[:].rearrange("p (g s r) -> p g r s", s=8, r=PACK),
        )
        nc.vector.tensor_copy(
            key_scale[:].rearrange("p (r s) -> p s r", r=PACK), key_bytes[:].indirect(token_list[:])
        )

        got_notes = sb("got_notes", [P, PACK, I], BF16)
        for t in range(PACK):
            listed = note_pool[t][:].indirect(note_list[:])
            if t % 2 == 1:
                nc.vector.tensor_copy(got_notes[:, t, :], listed)
            else:
                nc.scalar.activation(got_notes[:, t, :], listed, ACT.Copy)
        note_bf = sb("note_bf", [P, I * PACK], BF16)
        note_scale = sb("note_scale", [P, I], U8)

        q_bf = [sb(f"q_bf{n}", [P, Q * PACK], BF16) for n in range(2)]
        q_codes = [sb(f"q_codes{n}", [P, Q], U32) for n in range(2)]
        q_scale = [sb(f"q_scale{n}", [P, Q], U8) for n in range(2)]
        nc.scalar.copy(
            q_bf[0][:].rearrange("p (c i t) -> p c t i", i=4, t=PACK),
            q_raw[0][:].rearrange("p t (c i) -> p c t i", i=4),
        )
        nc.vector.tensor_copy(
            note_bf[:].rearrange("p (r g s t) -> p g r s t", r=PACK, s=2, t=PACK),
            got_notes[:].rearrange("p t (g s r) -> p g r s t", s=2, r=PACK),
        )
        for copy, first in ((nc.vector.tensor_copy, 0), (nc.scalar.copy, P)):
            copy(
                q_bf[1][:, first * PACK : (first + P) * PACK].rearrange("p (c i t) -> p c t i", i=4, t=PACK),
                q_raw[1][:, :, first : first + P].rearrange("p t (c i) -> p c t i", i=4),
            )
        nc.vector.quantize_mx(q_codes[0][:].bitcast(FP8X4), q_scale[0][:], q_bf[0][:])
        note_codes = sb("note_codes", [P, I], U32, tag="q_bf0")
        nc.vector.quantize_mx(note_codes[:].bitcast(FP8X4), note_scale[:], note_bf[:])
        nc.vector.quantize_mx(q_codes[1][:].bitcast(FP8X4), q_scale[1][:], q_bf[1][:])

        val_bf = {}
        val_scale = [sb(f"val_scale{b}", [P, P], U8) for b in range(BLOCKS)]
        val_codes = {}
        turned = {}
        turn_banks = ("scores0", "scores1", "turned2", "turned3")

        def gather_values(b, on_scalar, reuse):
            got_vals = sb(f"got_vals{b}", [P, I], BF16, tag=reuse)
            listed = val_pool[b][:].indirect(token_list[:])
            if on_scalar:
                nc.scalar.activation(got_vals[:], listed, ACT.Copy)
            else:
                nc.vector.tensor_copy(got_vals[:], listed)
            return got_vals

        def turn_values(b, got_vals):
            pairs = got_vals[:].bitcast(F32)
            turned[b] = psum.tile([P, 2, P], F32, name=f"turned{b}", tag=turn_banks[b])
            for u in range(2):
                nc.tensor.transpose(turned[b][:, u, :], pairs[:, u : I // 2 : 2], identity[:])

        def weave_values(b, on_scalar, reuse=None):
            val_bf[b] = sb(f"val_bf{b}", [P, P * PACK], BF16, tag=reuse)
            woven = val_bf[b][:].bitcast(F32).rearrange("p (e u) -> p e u", u=2)
            if on_scalar:
                nc.scalar.copy(woven, turned[b][:].rearrange("p u e -> p e u"))
            else:
                nc.vector.tensor_copy(woven, turned[b][:].rearrange("p u e -> p e u"))

        def quantise_values(b, reuse=None):
            val_codes[b] = sb(f"val_codes{b}", [P, P], U32, tag=reuse)
            nc.vector.quantize_mx(val_codes[b][:].bitcast(FP8X4), val_scale[b][:], val_bf[b][:])

        weight = sb("weight", [P, Q, PACK], F32)
        weight_codes = sb("weight_codes", [P, Q], U32)
        weight_scale = sb("weight_scale", [P, Q], U8)
        scores = [psum.tile([P, PACK, P], F32, name=f"scores{h}", tag=f"scores{h}") for h in range(HALVES)]
        for h in range(HALVES):
            rows = slice(h * P, (h + 1) * P)
            for r in range(PACK):
                slots = slice(r * P, (r + 1) * P)
                nc.tensor.matmul_mx(
                    scores[h][:, r, :],
                    lhsT=key_codes[:, slots].bitcast(FP4X4),
                    lhsT_scale=key_scale[:, slots],
                    rhs=q_codes[0][:, rows].bitcast(FP8X4),
                    rhs_scale=q_scale[0][:, rows],
                    start=(r == 0),
                    stop=False,
                )
        got0 = gather_values(0, False, "q_bf1")
        weight_bf = sb("weight_bf", [P, Q, PACK], BF16, tag="val_pool0")
        for h in range(HALVES):
            rows = slice(h * P, (h + 1) * P)
            for r in range(PACK):
                slots = slice(r * P, (r + 1) * P)
                nc.tensor.matmul_mx(
                    scores[h][:, r, :],
                    lhsT=note_codes[:, slots].bitcast(FP8X4),
                    lhsT_scale=note_scale[:, slots],
                    rhs=q_codes[1][:, rows].bitcast(FP8X4),
                    rhs_scale=q_scale[1][:, rows],
                    start=False,
                    stop=(r == PACK - 1),
                )
            nc.scalar.activation(weight[:, rows, :], scores[h][:].rearrange("p r q -> p q r"), ACT.Sigmoid)
            nc.vector.tensor_tensor(
                weight_bf[:, rows, :],
                weight[:, rows, :],
                slot_factor[:].unsqueeze(1).to_broadcast([P, P, PACK]),
                ALU.mult,
            )
        turn_values(0, got0)
        weave_values(0, True)
        quantise_values(0)
        nc.vector.quantize_mx(
            weight_codes[:].bitcast(FP8X4), weight_scale[:], weight_bf[:].rearrange("p q r -> p (q r)")
        )

        result = [sb(f"result{b}", [P, M], F32) for b in range(BLOCKS)]
        read = {}

        def read_values(b, reuse=None):
            sums = psum.tile([P, Q], F32, name=f"sums{b}", tag=f"sums{b % 2}")
            nc.tensor.matmul_mx(
                sums[:],
                lhsT=val_codes[b][:].bitcast(FP8X4),
                lhsT_scale=val_scale[b][:],
                rhs=weight_codes[:].bitcast(FP8X4),
                rhs_scale=weight_scale[:],
                start=True,
                stop=True,
            )
            read[b] = sb(f"read{b}", [P, Q], F32, tag=reuse)
            nc.scalar.copy(read[b][:], sums[:])

        def place(b):
            nc.scalar.activation(placed[b % 2][:].indirect(column_list[:]), read[b][:], ACT.Copy)

        def update(b, store_parts):
            parts = [slice(0, M // 2), slice(M // 2, M)]
            larger = [sb(f"larger{b}_{n}", [P, M // 2], F32) for n in range(2)]
            for n, cols in enumerate(parts):
                nc.vector.tensor_tensor(larger[n][:], placed[b % 2][:, cols], old_rows[b][:, cols], ALU.max)
            ends = (M // 2, 3 * M // 4, M) if store_parts else (M // 2, M)
            for first, end in zip((0,) + ends, ends):
                cols = slice(first, end)
                n = first // (M // 2)
                within = slice(first - n * (M // 2), end - n * (M // 2))
                nc.vector.scalar_tensor_tensor(
                    result[b][:, cols], old_rows[b][:, cols], 0.25, larger[n][:, within], ALU.mult, ALU.add
                )
                if store_parts:
                    nc.sync.dma_start(out[b * P : (b + 1) * P, cols], result[b][:, cols])
            if not store_parts:
                nc.sync.dma_start(out[b * P : (b + 1) * P, :], result[b][:])

        turn_values(1, gather_values(1, True, "q_bf0"))
        read_values(0, "val_pool1")
        place(0)
        turn_values(2, gather_values(2, False, "val_pool0"))
        weave_values(1, False, "val_pool2")
        quantise_values(1)
        weave_values(2, True)
        read_values(1, "val_pool0")
        place(1)
        turn_values(3, gather_values(3, False, None))
        quantise_values(2, "val_pool3")
        weave_values(3, True)
        read_values(2, "got_vals3")
        update(0, False)
        place(2)
        quantise_values(3, "larger0_1")
        update(1, False)
        read_values(3)
        place(3)
        update(2, False)
        update(3, True)
